import numpy as np
import ml_dtypes


def mxq(x, axis, fmt="e4m3"):
    dtype, down = {"e4m3": (ml_dtypes.float8_e4m3fn, 7), "e5m2": (ml_dtypes.float8_e5m2, 14)}[fmt]
    v = np.moveaxis(np.asarray(x, np.float32).astype(ml_dtypes.bfloat16).astype(np.float64), axis, -1)
    blocks = v.reshape(v.shape[:-1] + (-1, 32))
    amax = np.abs(blocks).max(-1, keepdims=True)
    byte = np.maximum(np.where(amax > 0, np.frexp(amax)[1] - 1 + 127, 0) - down, 1)
    scale = np.exp2(byte - 127.0)
    codes = (blocks / scale).astype(np.float32).astype(dtype).astype(np.float64)
    return np.moveaxis((codes * scale).reshape(v.shape), -1, axis)


WIDE = False


def mx_kscale(k):
    if not WIDE:
        return np.ones(k)
    levels = np.array([10, -10, 5, -5, 0])
    if k % 512:
        return np.exp2(np.random.permutation(np.resize(levels, k // 32))).repeat(32)
    a = np.empty((k // 512, 16))
    for p in range(k // 512):
        a[p, :8] = np.random.permutation(np.resize(levels, 8))
        for g in range(8):
            far = levels[np.abs(levels - a[p, g]) >= 10]
            a[p, g + 8] = far[np.random.randint(len(far))]
    return np.exp2(a.ravel()).repeat(32)


def f64(x):
    return np.asarray(x).astype(np.float64)


def striped(idx):
    return np.tile(idx.reshape(-1, 16).T, (8, 1)).astype(np.uint16)


def unstriped(offs):
    return offs[:16].T.reshape(-1).astype(np.int64)


E2M1 = np.array([0.0, 0.5, 1.0, 1.5, 2.0, 3.0, 4.0, 6.0, -0.0, -0.5, -1.0, -1.5, -2.0, -3.0, -4.0, -6.0])


def pack_weight(w, fmt):
    k, n = w.shape
    w = f64(np.asarray(w, np.float32).astype(ml_dtypes.bfloat16)).reshape(k // 32, 32, n)
    amax = np.abs(w).max(1)
    if fmt == "e4m3":
        byte = np.frexp(amax)[1] - 1 + 127 - 7
    else:
        mant, ex = np.frexp(amax / 6.0)
        byte = np.where(mant > 0.5, ex, ex - 1) + 127
    byte = np.clip(np.where(amax > 0, byte, 1), 1, 254)
    scaled = (w * np.exp2(127.0 - byte)[:, None, :]).reshape(k, n).astype(np.float32)
    by_word = np.ascontiguousarray(scaled.reshape(k // 512, 128, 4, n).transpose(0, 1, 3, 2))
    if fmt == "e4m3":
        words = by_word.astype(ml_dtypes.float8_e4m3fn).view(np.uint8)
    else:
        c = by_word.astype(ml_dtypes.float4_e2m1fn).view(np.uint8) & 0xF
        words = (c[..., 0::2] | (c[..., 1::2] << 4)).reshape(k // 512, 128, 2 * n)
    return np.ascontiguousarray(words), np.ascontiguousarray(byte.astype(np.uint8).reshape(k // 512, 16, n))


def unpack_weight(words, scales, fmt):
    g, _, n = scales.shape
    words = np.ascontiguousarray(words).reshape(g, 128, n, -1)
    if fmt == "e4m3":
        vals = words.view(ml_dtypes.float8_e4m3fn).astype(np.float64)
    else:
        nib = np.empty((g, 128, n, 4), np.uint8)
        nib[..., 0::2] = words & 0xF
        nib[..., 1::2] = words >> 4
        vals = E2M1[nib]
    vals = vals * np.repeat(np.exp2(scales.astype(np.float64) - 127.0), 8, axis=1)[..., None]
    return vals.transpose(0, 1, 3, 2).reshape(g * 512, n)


def gelu(v):
    return 0.5 * v * (1.0 + np.tanh(np.sqrt(2.0 / np.pi) * (v + 0.044715 * v**3)))


def striped8(idx):
    return np.concatenate([v.reshape(-1, 16).T for v in idx]).astype(np.uint16)


def unstriped8(offs):
    return np.stack([offs[16 * g:16 * g + 16].T.reshape(-1) for g in range(8)]).astype(np.int64)


def heads(h, wgt, idx8):
    r = np.arange(h.shape[0])
    return wgt[r // 4 % 128] * h[r[:, None], idx8[r % 512 // 64]]


def put_heads(h, wgs, idx8, t2):
    r = np.arange(h.shape[0])
    page = np.zeros((h.shape[0], t2))
    page[r[:, None], idx8[r % 512 // 64]] = wgs[r // 4 % 128] * h
    return page


K, H, N, T, S, P, T2 = 1536, 1024, 512, 4096, 1024, 1024, 2048

def setup_inputs():
    n = np.random.standard_normal
    s = mx_kscale(K)[:, None]
    u = mx_kscale(H)[:, None]
    u2 = mx_kscale(N)[:, None]
    d = {}
    d["tab_words"], d["tab_scales"] = pack_weight(n((K, T)) * s, "e4m3")
    d["offs"] = striped(np.random.permutation(T)[:S])
    d["w1"] = (n((K, H)) / K**0.5 / s).astype(np.float32)
    d["lim"] = (0.4 + 0.6 * n((H, S))).astype(np.float32)
    d["ga"] = (np.exp(0.3 * n(H)) * u[:, 0]).astype(np.float32)
    d["offs2"] = striped8(np.stack([np.random.permutation(T2)[:S] for _ in range(8)]))
    d["wgs"] = np.repeat(np.random.uniform(0.5, 2.0, (8, S)), 16, axis=0).astype(np.float32)
    d["offs3"] = striped8(np.stack([np.random.permutation(T2)[:P] for _ in range(8)]))
    d["wgt"] = np.repeat(np.random.uniform(0.5, 2.0, (8, P)), 16, axis=0).astype(np.float32)
    d["clim"] = (0.8 * n((H, P)) * u).astype(np.float32)
    d["w2_words"], d["w2_scales"] = pack_weight(n((H, N)) / H**0.5 / u, "e2m1")
    d["gf"] = (np.exp(0.3 * n(N)) * u2[:, 0]).astype(np.float32)
    d["w3"] = (n((N, N)) / N**0.5 / u2).astype(np.float32)
    return d

def reference(tab_words, tab_scales, offs, w1, lim, ga, offs2, wgs, offs3, wgt, clim, w2_words, w2_scales, gf, w3):
    v = unpack_weight(tab_words, tab_scales, "e4m3")[:, unstriped(offs)]
    a = mxq(f64(w1), 0, "e4m3").T @ v
    h = f64(ga)[:, None] * np.minimum(a, f64(lim))
    page = put_heads(h, f64(wgs), unstriped8(offs2), T2)
    x = heads(page, f64(wgt), unstriped8(offs3))
    z = x + f64(clim)
    w2 = unpack_weight(w2_words, w2_scales, "e2m1")
    f = np.tanh(w2.T @ mxq(z, 0, "e4m3"))
    fg = f64(gf)[:, None] * f
    return (mxq(f64(w3), 0, "e4m3").T @ mxq(fg, 0, "e4m3")) + f

@@ -1,0 +1,367 @@
+from contextlib import ExitStack
+
+import concourse.mybir as mybir
+from concourse.masks import make_identity
+
+K, H, N, T, S, T2 = 1536, 1024, 512, 4096, 1024, 2048
+FLOPS = 2 * (K * H * S + H * N * S + N * N * S)
+
+F32 = mybir.dt.float32
+BF16 = mybir.dt.bfloat16
+I32 = mybir.dt.int32
+U32 = mybir.dt.uint32
+U16 = mybir.dt.uint16
+U8 = mybir.dt.uint8
+E4M3 = mybir.dt.float8_e4m3fn_x4
+E2M1 = mybir.dt.float4_e2m1fn_x4
+ALU = mybir.AluOpType
+ACT = mybir.ActivationFunctionType
+
+P = 128
+PACK = 4
+PASS = P * PACK
+BANK = 512
+LIST = 16
+KP = K // PASS
+HP = H // PASS
+CHUNKS = (128, 256, 256, 256, 128)
+
+
+def tile_list_moromi_panel_aroma_kernel(
+    tc, tab_words, tab_scales, offs, w1, lim, ga, offs2, wgs, offs3, wgt, clim, w2_words, w2_scales, gf, w3, out
+):
+    nc = tc.nc
+    with ExitStack() as ctx:
+        lists = ctx.enter_context(tc.tile_pool(name="lists", bufs=1))
+        keep = ctx.enter_context(tc.tile_pool(name="keep", bufs=1))
+        ring = ctx.enter_context(tc.tile_pool(name="ring", bufs=2))
+        psum = ctx.enter_context(tc.psum_pool(name="psum", bufs=2))
+
+        def big(shape, dtype, name):
+            return ring.tile(shape, dtype, name=name, tag="big", bufs=3, align_bytes=64)
+
+        def row(shape, name):
+            return ring.tile(shape, F32, name=name, tag="row", bufs=4, align_bytes=64)
+
+        def raw_weight(name):
+            return ring.tile([P, PACK, PASS], F32, name=name, tag="raw", bufs=3, align_bytes=64)
+
+        def early(shape, dtype, name):
+            return ring.tile(shape, dtype, name=name, tag="early", bufs=4, align_bytes=64)
+
+        def low_slot(shape, dtype, name):
+            return ring.tile(shape, dtype, name=name, tag="low", bufs=3, align_bytes=64)
+
+        def acc_bank(shape, name):
+            return psum.tile(shape, F32, name=name, tag="acc", bufs=4)
+
+        def clock(ap):
+            tick = ring.tile([P, 1], F32, name="tick", tag="tick")
+            nc.gpsimd.tensor_copy(tick[:], ap)
+
+        def cols(lst, j0, width):
+            return lst[:, j0 // LIST : (j0 + width) // LIST]
+
+        tab_sc = early([P, T], U8, "tab_sc")
+        w2_sc_raw = ring.tile([P, HP, N], U8, name="w2_sc_raw", tag="fg_grouped", align_bytes=64)
+        nc.vector.memset(tab_sc[:].bitcast(I32), 0)
+        nc.vector.memset(w2_sc_raw[:].rearrange("p a c -> p (a c)").bitcast(I32), 0)
+
+        idx = lists.tile([P, S // LIST], U16, name="idx")
+        idx2 = lists.tile([P, S // LIST], U16, name="idx2")
+        idx3 = lists.tile([P, S // LIST], U16, name="idx3")
+        nc.sync.dma_start(idx[:], offs)
+
+        w2_raw = ring.tile([P, HP, 2 * N], U8, name="w2_raw", tag="fg_planes", align_bytes=64)
+        ga_sb = keep.tile([P, HP, PACK], F32, name="ga_sb")
+        gf_sb = keep.tile([P, PACK], F32, name="gf_sb")
+        pages = [keep.tile([P, T2], F32, name="page%d" % t) for t in range(PACK)]
+        for t in range(PACK - 1):
+            nc.gpsimd.memset(pages[t][:], 0.0)
+        nc.vector.memset(pages[PACK - 1][:], 0.0)
+        ident = keep.tile([P, P], F32, name="ident")
+        make_identity(nc, ident[:])
+
+        def load_table(a):
+            words = big([P, T], I32, "tab%d" % a)
+            nc.sync.dma_start(words[:], tab_words[a].rearrange("p t i -> p (t i)").bitcast(I32))
+            return words
+
+        def load_weight(rows, name):
+            raw = raw_weight(name)
+            nc.sync.dma_start(raw[:], rows.rearrange("(p i) c -> p i c", i=PACK))
+            return raw
+
+        def w1_rows(b, a):
+            return w1[a * PASS : (a + 1) * PASS, b * PASS : (b + 1) * PASS]
+
+        lim_v = lim.rearrange("(b p i) j -> b p i j", b=HP, i=PACK)
+        clim_v = clim.rearrange("(b p i) j -> b p i j", b=HP, i=PACK)
+        tab = {}
+        w1_raw = {}
+        tab[0] = load_table(0)
+        tab_sc_rows = early([P, T // 4], I32, "tab_sc_rows")
+        for q in range(4):
+            rows = slice(32 * q, 32 * q + 4 * KP)
+            nc.sync.dma_start(tab_sc_rows[rows, :], tab_scales[:, 4 * q : 4 * q + 4, :].bitcast(I32))
+            nc.vector.tensor_copy(tab_sc[rows, :].bitcast(I32), tab_sc_rows[rows, :])
+        nc.sync.dma_start(ga_sb[:], ga.rearrange("(b p i) -> p b i", b=HP, i=PACK))
+        warm = keep.tile([P, 1], F32, name="warm")
+        nc.scalar.activation(warm[:], ga_sb[:, 0, 0:1], ACT.Tanh)
+        w1_raw[0, 0] = load_weight(w1_rows(0, 0), "w1_00")
+        tab[1] = load_table(1)
+        nc.sync.dma_start(w2_raw[:].bitcast(I32), w2_words.rearrange("a p c -> p a c").bitcast(I32))
+        w2_sc_rows = ring.tile([P, HP, N // 4], I32, name="w2_sc_rows", tag="fg_grouped", align_bytes=64)
+        for q in range(4):
+            rows = slice(32 * q, 32 * q + 4)
+            nc.sync.dma_start(
+                w2_sc_rows[rows, :, :], w2_scales[:, 4 * q : 4 * q + 4, :].rearrange("a r c -> r a c").bitcast(I32)
+            )
+            nc.vector.tensor_copy(w2_sc_raw[rows, :, :].bitcast(I32), w2_sc_rows[rows, :, :])
+        nc.sync.dma_start(gf_sb[:], gf.rearrange("(p i) -> p i", i=PACK))
+        w1_raw[0, 1] = load_weight(w1_rows(0, 1), "w1_01")
+        tab[2] = load_table(2)
+        w1_raw[0, 2] = load_weight(w1_rows(0, 2), "w1_02")
+        wgs_sb = keep.tile([P, S], F32, name="wgs_sb")
+        wgt_sb = keep.tile([P, S], F32, name="wgt_sb")
+        lim_sb = {}
+        lim_sb[0, 0] = row([P, S], "lim00")
+        for h in range(2):
+            half = slice(h * BANK, (h + 1) * BANK)
+            nc.sync.dma_start(wgs_sb[:, half], wgs[:, half])
+            nc.sync.dma_start(lim_sb[0, 0][:, half], lim_v[0, :, 0, half])
+            if h == 0:
+                nc.sync.dma_start(idx2[:], offs2)
+        for t in range(1, PACK):
+            lim_sb[0, t] = row([P, S], "lim0%d" % t)
+            nc.sync.dma_start(lim_sb[0, t][:], lim_v[0, :, t, :])
+        nc.sync.dma_start(idx3[:], offs3)
+        nc.sync.dma_start(wgt_sb[:], wgt)
+
+        v_sc = keep.tile([P, S], U8, name="v_sc", align_bytes=64)
+        nc.vector.tensor_copy(v_sc[:], tab_sc[:].indirect(idx[:]))
+        v_codes = {}
+        for a in range(KP):
+            for h in range(2):
+                v_codes[a, h] = keep.tile([P, BANK], U32, name="v%d%d" % (a, h), align_bytes=64)
+                nc.vector.tensor_copy(
+                    v_codes[a, h][:], tab[a][:].bitcast(U32).indirect(cols(idx, h * BANK, BANK))
+                )
+
+        def round_weight_slice(raw, t):
+            grouped = ring.tile([P, P, PACK], BF16, name="grouped", tag="grouped", bufs=12, align_bytes=64)
+            nc.scalar.copy(grouped[:], raw[:].rearrange("p i (q t) -> p t q i", t=PACK)[:, t, :, :])
+            return grouped
+
+        def quantise_weight_slice(grouped, name):
+            codes = keep.tile([P, P], U32, name=name + "c", align_bytes=64)
+            scales = keep.tile([P, P], U8, name=name + "s", align_bytes=64)
+            nc.vector.quantize_mx(
+                out=codes[:].bitcast(E4M3), scales=scales[:], in_=grouped[:].rearrange("p q i -> p (q i)")
+            )
+            return codes, scales
+
+        w1_q = {}
+        gain = {}
+        for t in range(PACK):
+            for a in range(KP):
+                w1_q[0, t, a] = quantise_weight_slice(round_weight_slice(w1_raw[0, a], t), "w1q0%d%d" % (t, a))
+            gain[0, t] = early([P, S], F32, "gain0%d" % t)
+            for h in range(2):
+                half = slice(h * BANK, (h + 1) * BANK)
+                nc.scalar.activation(gain[0, t][:, half], wgs_sb[:, half], ACT.Copy, scale=ga_sb[:, 0, t : t + 1])
+
+        w2_codes = keep.tile([P, HP, PACK, P, 2], U8, name="w2_codes", align_bytes=64)
+        w2_sc = keep.tile([P, HP, PACK, P], U8, name="w2_sc", align_bytes=64)
+        for b in range(HP):
+            nc.vector.tensor_copy(
+                w2_codes[:, b, :, :, :], w2_raw[:, b, :].rearrange("p (q t e) -> p t q e", t=PACK, e=2)
+            )
+        nc.vector.tensor_copy(w2_sc[:], w2_sc_raw[:].rearrange("p a (q t) -> p a t q", t=PACK))
+
+        for a in range(KP):
+            w1_raw[1, a] = load_weight(w1_rows(1, a), "w1_1%d" % a)
+        lim1 = big([P, PACK, S], F32, "lim1")
+        nc.sync.dma_start(lim1[:], lim_v[1])
+        for t in range(PACK):
+            lim_sb[1, t] = lim1[:, t, :]
+        clim_sb = {}
+        clim_sb[0] = big([P, PACK, S], F32, "clim0")
+        nc.sync.dma_start(clim_sb[0][:], clim_v[0])
+        clim_sb[1] = big([P, PACK, S], F32, "clim1")
+        nc.sync.dma_start(clim_sb[1][:], clim_v[1])
+
+        w1_rounded = {}
+        for t in range(PACK):
+            for a in range(KP):
+                w1_rounded[t, a] = round_weight_slice(w1_raw[1, a], t)
+        for t0 in range(0, PACK, 2):
+            two = ring.tile([P, 2, S], F32, name="gain1%d" % t0, tag="raw", bufs=3, align_bytes=64)
+            for t in range(t0, t0 + 2):
+                gain[1, t] = two[:, t - t0, :]
+                nc.scalar.activation(gain[1, t], wgs_sb[:], ACT.Copy, scale=ga_sb[:, 1, t : t + 1])
+        w3_raw = load_weight(w3, "w3_raw")
+
+        def capped(b, t):
+            low = low_slot([P, S], F32, "low")
+            for h in range(2):
+                half = slice(h * BANK, (h + 1) * BANK)
+                acc = acc_bank([P, BANK], "acc1")
+                for a in range(KP):
+                    codes, scales = w1_q[b, t, a]
+                    nc.tensor.matmul_mx(
+                        out=acc[:],
+                        lhsT=codes[:].bitcast(E4M3),
+                        lhsT_scale=scales[:],
+                        rhs=v_codes[a, h][:].bitcast(E4M3),
+                        rhs_scale=v_sc[4 * a : P, half],
+                        start=(a == 0),
+                        stop=(a == KP - 1),
+                    )
+                nc.vector.tensor_tensor(low[:, half], acc[:], lim_sb[b, t][:, half], ALU.min)
+            if (b, t) == (0, 0):
+                clock(low[:, 0:1])
+            return low, gain[b, t]
+
+        def put(t, low, factor, pieces):
+            width = S // pieces
+            for j0 in range(0, S, width):
+                span = slice(j0, j0 + width)
+                nc.vector.tensor_tensor(
+                    pages[t][:].indirect(cols(idx2, j0, width)), low[:, span], factor[:, span], ALU.mult
+                )
+
+        def pick(t, dst, j0, width):
+            nc.vector.tensor_tensor(
+                dst, pages[t][:].indirect(cols(idx3, j0, width)), wgt_sb[:, j0 : j0 + width], ALU.mult
+            )
+
+        z_q = {}
+
+        def round_z(b, j0, x_blocks):
+            total = psum.tile([P, PACK, P], F32, name="total", tag="total")
+            for t in range(PACK):
+                nc.tensor.matmul(
+                    total[:, t, :], clim_sb[b][:, t, j0 : j0 + P], ident[:],
+                    start=(t == 0), stop=False, is_transpose=True,
+                )
+            for t in range(PACK):
+                nc.tensor.matmul(
+                    total[:, t, :], x_blocks[t], ident[:], start=False, stop=(t == PACK - 1), is_transpose=True
+                )
+            z_rows = ring.tile([P, 2, P, 2], BF16, name="z_rows", tag="z_rows", align_bytes=64)
+            nc.scalar.copy(z_rows[:], total[:].rearrange("j (u e) p -> j u p e", e=2))
+            pairs = psum.tile([P, 2, P], F32, name="pairs", tag="pairs")
+            z_words = z_rows[:].rearrange("j u p e -> j (u p e)").bitcast(F32)
+            for u in range(2):
+                nc.tensor.transpose(pairs[:, u, :], z_words[:, u * P : (u + 1) * P], ident[:])
+            z_grouped = ring.tile([P, P * PACK], BF16, name="z_grouped", tag="z_grouped", bufs=8, align_bytes=64)
+            nc.scalar.copy(
+                z_grouped[:].bitcast(F32).rearrange("p (j u) -> p j u", u=2), pairs[:].rearrange("p u j -> p j u")
+            )
+            return z_grouped
+
+        def quantise_z(b, j0, z_grouped, codes):
+            scales = keep.tile([P, P], U8, name="zs%d_%d" % (b, j0), align_bytes=64)
+            nc.vector.quantize_mx(out=codes.bitcast(E4M3), scales=scales[:], in_=z_grouped[:])
+            z_q[b, j0] = (codes, scales)
+
+        order = [(b, t) for b in range(HP) for t in range(PACK)]
+        x0 = {}
+        w3_q = {}
+        ready = capped(0, 0)
+        for n, (b, t) in enumerate(order):
+            current = ready
+            if n + 1 < len(order):
+                if order[n + 1][0] == 1:
+                    for a in range(KP):
+                        tn = order[n + 1][1]
+                        w1_q[1, tn, a] = quantise_weight_slice(w1_rounded[tn, a], "w1q1%d%d" % (tn, a))
+                ready = capped(*order[n + 1])
+            put(t, current[0], current[1], 2 if n == 0 else 1)
+            if 1 <= n <= PACK:
+                x0[n - 1] = row([P, S], "x0%d" % (n - 1))
+                pick(n - 1, x0[n - 1][:], 0, S)
+            if n == PACK:
+                z0 = {j0: round_z(0, j0, [x0[i][:, j0 : j0 + P] for i in range(PACK)]) for j0 in range(0, S, P)}
+            if n == len(order) - 2:
+                z0_codes = ring.tile([P, S], U32, name="z0_codes", tag="row", bufs=4, align_bytes=64)
+                z1_codes = ring.tile([P, S], U32, name="z1_codes", tag="row", bufs=4, align_bytes=64)
+                for j0 in range(0, S, P):
+                    quantise_z(0, j0, z0[j0], z0_codes[:, j0 : j0 + P])
+                for i in range(PACK):
+                    w3_q[i] = quantise_weight_slice(round_weight_slice(w3_raw, i), "w3q%d" % i)
+                x_first = row([P, PACK, CHUNKS[0]], "x1")
+                for i in range(PACK - 1):
+                    pick(i, x_first[:, i, :], 0, CHUNKS[0])
+
+        out_v = out.rearrange("(p t) j -> p t j", t=PACK)
+
+        def stage_pick(j0, width):
+            x = x_first if j0 == 0 else row([P, PACK, width], "x1")
+            for t in range(PACK - 1 if j0 == 0 else 0, PACK):
+                pick(t, x[:, t, :], j0, width)
+            for u in range(0, width, P):
+                rounded = round_z(1, j0 + u, [x[:, t, u : u + P] for t in range(PACK)])
+                quantise_z(1, j0 + u, rounded, z1_codes[:, j0 + u : j0 + u + P])
+            if j0 == 0:
+                clock(x[:, 3, 0:1])
+
+        def stage_features(j0, width):
+            f = early([P, PACK, width], F32, "f")
+            for u in range(0, width, P):
+                acc = acc_bank([P, PACK, P], "acc2")
+                for t in range(PACK):
+                    for b in range(HP):
+                        codes, scales = z_q[b, j0 + u]
+                        nc.tensor.matmul_mx(
+                            out=acc[:, t, :],
+                            lhsT=w2_codes[:, b, t, :, :].rearrange("p q e -> p (q e)").bitcast(E2M1),
+                            lhsT_scale=w2_sc[:, b, t, :],
+                            rhs=codes.bitcast(E4M3),
+                            rhs_scale=scales[:],
+                            start=(b == 0),
+                            stop=(b == HP - 1),
+                        )
+                nc.scalar.activation(f[:, :, u : u + P], acc[:], ACT.Tanh)
+            fg_planes = ring.tile([P, PACK, width], BF16, name="fg_planes", tag="fg_planes", align_bytes=64)
+            for t in range(PACK):
+                nc.scalar.activation(fg_planes[:, t, :], f[:, t, :], ACT.Copy, scale=gf_sb[:, t : t + 1])
+            fg_grouped = ring.tile([P, width, PACK], BF16, name="fg_grouped", tag="fg_grouped", align_bytes=64)
+            nc.scalar.copy(fg_grouped[:], fg_planes[:].rearrange("p t j -> p j t"))
+            return f, fg_grouped
+
+        def stage_out(j0, width, f, fg_grouped):
+            codes = ring.tile([P, width], U32, name="fg_codes", tag="fg_codes", align_bytes=64)
+            scales = ring.tile([P, width], U8, name="fg_scales", tag="fg_scales", align_bytes=64)
+            nc.vector.quantize_mx(
+                out=codes[:].bitcast(E4M3), scales=scales[:], in_=fg_grouped[:].rearrange("p j t -> p (j t)")
+            )
+            result = low_slot([P, PACK, width], F32, "result")
+            per_bank = BANK // width
+            for t0 in range(0, PACK, per_bank):
+                acc = acc_bank([P, per_bank, width], "acc3")
+                for t in range(t0, t0 + per_bank):
+                    nc.tensor.matmul_mx(
+                        out=acc[:, t - t0, :],
+                        lhsT=w3_q[t][0][:].bitcast(E4M3),
+                        lhsT_scale=w3_q[t][1][:],
+                        rhs=codes[:].bitcast(E4M3),
+                        rhs_scale=scales[:],
+                        start=True,
+                        stop=True,
+                    )
+                nc.vector.tensor_tensor(
+                    result[:, t0 : t0 + per_bank, :], acc[:], f[:, t0 : t0 + per_bank, :], ALU.add
+                )
+            nc.sync.dma_start(out_v[:, :, j0 : j0 + width], result[:])
+
+        starts = [sum(CHUNKS[:c]) for c in range(len(CHUNKS))]
+        made = {}
+        for c in range(len(CHUNKS) + 2):
+            if c < len(CHUNKS):
+                stage_pick(starts[c], CHUNKS[c])
+            if 1 <= c <= len(CHUNKS):
+                made[c - 1] = stage_features(starts[c - 1], CHUNKS[c - 1])
+            if c >= 2:
+                stage_out(starts[c - 2], CHUNKS[c - 2], *made[c - 2])

@@ -25,6 +25,9 @@ LIST = 16
 KP = K // PASS
 HP = H // PASS
 CHUNKS = (128, 256, 256, 256, 128)
+FUSE_EARLY = True
+FUSE_LATE = True
+VECTOR_GAIN_FROM = 640
 
 
 def tile_list_moromi_panel_aroma_kernel(
@@ -63,7 +66,7 @@ def tile_list_moromi_panel_aroma_kernel(
             return lst[:, j0 // LIST : (j0 + width) // LIST]
 
         tab_sc = early([P, T], U8, "tab_sc")
-        w2_sc_raw = ring.tile([P, HP, N], U8, name="w2_sc_raw", tag="fg_grouped", align_bytes=64)
+        w2_sc_raw = ring.tile([P, HP, N], U8, name="w2_sc_raw", tag="late", bufs=3, align_bytes=64)
         nc.vector.memset(tab_sc[:].bitcast(I32), 0)
         nc.vector.memset(w2_sc_raw[:].rearrange("p a c -> p (a c)").bitcast(I32), 0)
 
@@ -72,13 +75,12 @@ def tile_list_moromi_panel_aroma_kernel(
         idx3 = lists.tile([P, S // LIST], U16, name="idx3")
         nc.sync.dma_start(idx[:], offs)
 
-        w2_raw = ring.tile([P, HP, 2 * N], U8, name="w2_raw", tag="fg_planes", align_bytes=64)
+        w2_raw = ring.tile([P, HP, 2 * N], U8, name="w2_raw", tag="late", bufs=3, align_bytes=64)
         ga_sb = keep.tile([P, HP, PACK], F32, name="ga_sb")
         gf_sb = keep.tile([P, PACK], F32, name="gf_sb")
         pages = [keep.tile([P, T2], F32, name="page%d" % t) for t in range(PACK)]
-        for t in range(PACK - 1):
-            nc.gpsimd.memset(pages[t][:], 0.0)
-        nc.vector.memset(pages[PACK - 1][:], 0.0)
+        for t in range(PACK):
+            nc.vector.memset(pages[t][:], 0.0)
         ident = keep.tile([P, P], F32, name="ident")
         make_identity(nc, ident[:])
 
@@ -111,7 +113,7 @@ def tile_list_moromi_panel_aroma_kernel(
         w1_raw[0, 0] = load_weight(w1_rows(0, 0), "w1_00")
         tab[1] = load_table(1)
         nc.sync.dma_start(w2_raw[:].bitcast(I32), w2_words.rearrange("a p c -> p a c").bitcast(I32))
-        w2_sc_rows = ring.tile([P, HP, N // 4], I32, name="w2_sc_rows", tag="fg_grouped", align_bytes=64)
+        w2_sc_rows = ring.tile([P, HP, N // 4], I32, name="w2_sc_rows", tag="late", bufs=3, align_bytes=64)
         for q in range(4):
             rows = slice(32 * q, 32 * q + 4)
             nc.sync.dma_start(
@@ -148,35 +150,49 @@ def tile_list_moromi_panel_aroma_kernel(
                     v_codes[a, h][:], tab[a][:].bitcast(U32).indirect(cols(idx, h * BANK, BANK))
                 )
 
-        def round_weight_slice(raw, t):
-            grouped = ring.tile([P, P, PACK], BF16, name="grouped", tag="grouped", bufs=12, align_bytes=64)
-            nc.scalar.copy(grouped[:], raw[:].rearrange("p i (q t) -> p t q i", t=PACK)[:, t, :, :])
-            return grouped
+        def grouped_tile(name):
+            return ring.tile([P, PACK * PASS], BF16, name=name, tag="grouped", bufs=3, align_bytes=64)
 
-        def quantise_weight_slice(grouped, name):
-            codes = keep.tile([P, P], U32, name=name + "c", align_bytes=64)
-            scales = keep.tile([P, P], U8, name=name + "s", align_bytes=64)
-            nc.vector.quantize_mx(
-                out=codes[:].bitcast(E4M3), scales=scales[:], in_=grouped[:].rearrange("p q i -> p (q i)")
+        def round_weight_slice(grouped, raw, t):
+            nc.scalar.copy(
+                grouped[:, t * PASS : (t + 1) * PASS].rearrange("p (q i) -> p q i", i=PACK),
+                raw[:].rearrange("p i (q t) -> p t q i", t=PACK)[:, t, :, :],
             )
+
+        def operand(width, name):
+            codes = keep.tile([P, width], U32, name=name + "_codes", align_bytes=64)
+            scales = keep.tile([P, width], U8, name=name + "_scales", align_bytes=64)
             return codes, scales
 
-        w1_q = {}
+        def quantise(dst, c0, width, grouped):
+            codes, scales = dst
+            nc.vector.quantize_mx(
+                out=codes[:, c0 : c0 + width].bitcast(E4M3), scales=scales[:, c0 : c0 + width], in_=grouped
+            )
+
+        w1_q = {(b, a): operand(PASS, "w1q%d%d" % (b, a)) for b in range(HP) for a in range(KP)}
         gain = {}
-        for t in range(PACK):
-            for a in range(KP):
-                w1_q[0, t, a] = quantise_weight_slice(round_weight_slice(w1_raw[0, a], t), "w1q0%d%d" % (t, a))
-            gain[0, t] = early([P, S], F32, "gain0%d" % t)
-            for h in range(2):
-                half = slice(h * BANK, (h + 1) * BANK)
-                nc.scalar.activation(gain[0, t][:, half], wgs_sb[:, half], ACT.Copy, scale=ga_sb[:, 0, t : t + 1])
+        for a in range(KP):
+            grouped = grouped_tile("w1g0%d" % a)
+            for t in range(PACK):
+                round_weight_slice(grouped, w1_raw[0, a], t)
+                if a == KP - 1:
+                    quantise(w1_q[0, a], t * P, P, grouped[:, t * PASS : (t + 1) * PASS])
+                    gain[0, t] = early([P, S], F32, "gain0%d" % t)
+                    for h in range(2):
+                        half = slice(h * BANK, (h + 1) * BANK)
+                        nc.scalar.activation(
+                            gain[0, t][:, half], wgs_sb[:, half], ACT.Copy, scale=ga_sb[:, 0, t : t + 1]
+                        )
+            if a < KP - 1:
+                quantise(w1_q[0, a], 0, PASS, grouped[:])
 
         w2_codes = keep.tile([P, HP, PACK, P, 2], U8, name="w2_codes", align_bytes=64)
         w2_sc = keep.tile([P, HP, PACK, P], U8, name="w2_sc", align_bytes=64)
-        for b in range(HP):
-            nc.vector.tensor_copy(
-                w2_codes[:, b, :, :, :], w2_raw[:, b, :].rearrange("p (q t e) -> p t q e", t=PACK, e=2)
-            )
+        nc.vector.tensor_copy(
+            w2_codes[:].rearrange("p a t q e -> p a t (q e)").bitcast(U16),
+            w2_raw[:].bitcast(U16).rearrange("p a (q t) -> p a t q", t=PACK),
+        )
         nc.vector.tensor_copy(w2_sc[:], w2_sc_raw[:].rearrange("p a (q t) -> p a t q", t=PACK))
 
         for a in range(KP):
@@ -192,9 +208,10 @@ def tile_list_moromi_panel_aroma_kernel(
         nc.sync.dma_start(clim_sb[1][:], clim_v[1])
 
         w1_rounded = {}
-        for t in range(PACK):
-            for a in range(KP):
-                w1_rounded[t, a] = round_weight_slice(w1_raw[1, a], t)
+        for a in range(KP):
+            w1_rounded[a] = grouped_tile("w1g1%d" % a)
+            for t in range(PACK):
+                round_weight_slice(w1_rounded[a], w1_raw[1, a], t)
         for t0 in range(0, PACK, 2):
             two = ring.tile([P, 2, S], F32, name="gain1%d" % t0, tag="raw", bufs=3, align_bytes=64)
             for t in range(t0, t0 + 2):
@@ -208,19 +225,17 @@ def tile_list_moromi_panel_aroma_kernel(
                 half = slice(h * BANK, (h + 1) * BANK)
                 acc = acc_bank([P, BANK], "acc1")
                 for a in range(KP):
-                    codes, scales = w1_q[b, t, a]
+                    codes, scales = w1_q[b, a]
                     nc.tensor.matmul_mx(
                         out=acc[:],
-                        lhsT=codes[:].bitcast(E4M3),
-                        lhsT_scale=scales[:],
+                        lhsT=codes[:, t * P : (t + 1) * P].bitcast(E4M3),
+                        lhsT_scale=scales[:, t * P : (t + 1) * P],
                         rhs=v_codes[a, h][:].bitcast(E4M3),
                         rhs_scale=v_sc[4 * a : P, half],
                         start=(a == 0),
                         stop=(a == KP - 1),
                     )
                 nc.vector.tensor_tensor(low[:, half], acc[:], lim_sb[b, t][:, half], ALU.min)
-            if (b, t) == (0, 0):
-                clock(low[:, 0:1])
             return low, gain[b, t]
 
         def put(t, low, factor, pieces):
@@ -231,14 +246,17 @@ def tile_list_moromi_panel_aroma_kernel(
                     pages[t][:].indirect(cols(idx2, j0, width)), low[:, span], factor[:, span], ALU.mult
                 )
 
-        def pick(t, dst, j0, width):
-            nc.vector.tensor_tensor(
-                dst, pages[t][:].indirect(cols(idx3, j0, width)), wgt_sb[:, j0 : j0 + width], ALU.mult
-            )
+        def pick(t, dst, j0, width, fused):
+            picked = pages[t][:].indirect(cols(idx3, j0, width))
+            if fused:
+                nc.vector.tensor_tensor(dst, picked, wgt_sb[:, j0 : j0 + width], ALU.mult)
+            else:
+                nc.vector.tensor_copy(dst, picked)
+                nc.gpsimd.tensor_tensor(dst, dst, wgt_sb[:, j0 : j0 + width], ALU.mult)
 
         z_q = {}
 
-        def round_z(b, j0, x_blocks):
+        def round_z(b, j0, x_blocks, z_grouped):
             total = psum.tile([P, PACK, P], F32, name="total", tag="total")
             for t in range(PACK):
                 nc.tensor.matmul(
@@ -255,113 +273,133 @@ def tile_list_moromi_panel_aroma_kernel(
             z_words = z_rows[:].rearrange("j u p e -> j (u p e)").bitcast(F32)
             for u in range(2):
                 nc.tensor.transpose(pairs[:, u, :], z_words[:, u * P : (u + 1) * P], ident[:])
-            z_grouped = ring.tile([P, P * PACK], BF16, name="z_grouped", tag="z_grouped", bufs=8, align_bytes=64)
             nc.scalar.copy(
-                z_grouped[:].bitcast(F32).rearrange("p (j u) -> p j u", u=2), pairs[:].rearrange("p u j -> p j u")
+                z_grouped.bitcast(F32).rearrange("p (j u) -> p j u", u=2), pairs[:].rearrange("p u j -> p j u")
             )
-            return z_grouped
-
-        def quantise_z(b, j0, z_grouped, codes):
-            scales = keep.tile([P, P], U8, name="zs%d_%d" % (b, j0), align_bytes=64)
-            nc.vector.quantize_mx(out=codes.bitcast(E4M3), scales=scales[:], in_=z_grouped[:])
-            z_q[b, j0] = (codes, scales)
 
         order = [(b, t) for b in range(HP) for t in range(PACK)]
         x0 = {}
-        w3_q = {}
+        w3_q = operand(N, "w3q")
         ready = capped(0, 0)
         for n, (b, t) in enumerate(order):
             current = ready
+            if n == PACK - 1:
+                for a in range(KP):
+                    quantise(w1_q[1, a], 0, PASS, w1_rounded[a][:])
             if n + 1 < len(order):
-                if order[n + 1][0] == 1:
-                    for a in range(KP):
-                        tn = order[n + 1][1]
-                        w1_q[1, tn, a] = quantise_weight_slice(w1_rounded[tn, a], "w1q1%d%d" % (tn, a))
                 ready = capped(*order[n + 1])
             put(t, current[0], current[1], 2 if n == 0 else 1)
             if 1 <= n <= PACK:
                 x0[n - 1] = row([P, S], "x0%d" % (n - 1))
-                pick(n - 1, x0[n - 1][:], 0, S)
+                pick(n - 1, x0[n - 1][:], 0, S, FUSE_EARLY)
             if n == PACK:
-                z0 = {j0: round_z(0, j0, [x0[i][:, j0 : j0 + P] for i in range(PACK)]) for j0 in range(0, S, P)}
-            if n == len(order) - 2:
-                z0_codes = ring.tile([P, S], U32, name="z0_codes", tag="row", bufs=4, align_bytes=64)
-                z1_codes = ring.tile([P, S], U32, name="z1_codes", tag="row", bufs=4, align_bytes=64)
+                z0 = keep.tile([P, S * PACK], BF16, name="z0", align_bytes=64)
                 for j0 in range(0, S, P):
-                    quantise_z(0, j0, z0[j0], z0_codes[:, j0 : j0 + P])
+                    blocks = [x0[i][:, j0 : j0 + P] for i in range(PACK)]
+                    round_z(0, j0, blocks, z0[:, j0 * PACK : (j0 + P) * PACK])
+            if n == len(order) - 2:
+                z_q[0] = (
+                    ring.tile([P, S], U32, name="z0_codes", tag="row", bufs=4, align_bytes=64),
+                    keep.tile([P, S], U8, name="z0_scales", align_bytes=64),
+                )
+                z_q[1] = (
+                    low_slot([P, S], U32, "z1_codes"),
+                    keep.tile([P, S], U8, name="z1_scales", align_bytes=64),
+                )
+                quantise(z_q[0], 0, S, z0[:])
+                w3_grouped = grouped_tile("w3g")
                 for i in range(PACK):
-                    w3_q[i] = quantise_weight_slice(round_weight_slice(w3_raw, i), "w3q%d" % i)
-                x_first = row([P, PACK, CHUNKS[0]], "x1")
+                    round_weight_slice(w3_grouped, w3_raw, i)
+                quantise(w3_q, 0, N, w3_grouped[:])
+                x_first = row([P, S], "x1")
                 for i in range(PACK - 1):
-                    pick(i, x_first[:, i, :], 0, CHUNKS[0])
+                    pick(i, x_first[:, i * CHUNKS[0] : (i + 1) * CHUNKS[0]], 0, CHUNKS[0], True)
 
         out_v = out.rearrange("(p t) j -> p t j", t=PACK)
 
-        def stage_pick(j0, width):
-            x = x_first if j0 == 0 else row([P, PACK, width], "x1")
-            for t in range(PACK - 1 if j0 == 0 else 0, PACK):
-                pick(t, x[:, t, :], j0, width)
-            for u in range(0, width, P):
-                rounded = round_z(1, j0 + u, [x[:, t, u : u + P] for t in range(PACK)])
-                quantise_z(1, j0 + u, rounded, z1_codes[:, j0 + u : j0 + u + P])
-            if j0 == 0:
-                clock(x[:, 3, 0:1])
+        starts = [sum(CHUNKS[:c]) for c in range(len(CHUNKS))]
+        last = len(CHUNKS) - 1
+        x_tiles, z_tiles, f_tiles, y_banks = {}, {}, {}, {}
 
-        def stage_features(j0, width):
+        def stage_pick(c):
+            j0, width = starts[c], CHUNKS[c]
+            x = x_first if c == 0 else row([P, S], "x1")
+            x_tiles[c] = x
+            for t in range(PACK - 1 if c == 0 else 0, PACK):
+                pick(t, x[:, t * width : (t + 1) * width], j0, width, True)
+            z_tiles[c] = ring.tile([P, S], F32, name="z1", tag="late", bufs=3, align_bytes=64)
+            for u in range(0, width, P):
+                blocks = [x[:, t * width + u : t * width + u + P] for t in range(PACK)]
+                round_z(1, j0 + u, blocks, z_tiles[c][:, 2 * u : 2 * (u + P)].bitcast(BF16))
+
+        def stage_features(c):
+            j0, width = starts[c], CHUNKS[c]
+            quantise(z_q[1], j0, width, z_tiles[c][:, : 2 * width].bitcast(BF16))
             f = early([P, PACK, width], F32, "f")
+            f_tiles[c] = f
             for u in range(0, width, P):
                 acc = acc_bank([P, PACK, P], "acc2")
                 for t in range(PACK):
                     for b in range(HP):
-                        codes, scales = z_q[b, j0 + u]
+                        codes, scales = z_q[b]
                         nc.tensor.matmul_mx(
                             out=acc[:, t, :],
                             lhsT=w2_codes[:, b, t, :, :].rearrange("p q e -> p (q e)").bitcast(E2M1),
                             lhsT_scale=w2_sc[:, b, t, :],
-                            rhs=codes.bitcast(E4M3),
-                            rhs_scale=scales[:],
+                            rhs=codes[:, j0 + u : j0 + u + P].bitcast(E4M3),
+                            rhs_scale=scales[:, j0 + u : j0 + u + P],
                             start=(b == 0),
                             stop=(b == HP - 1),
                         )
                 nc.scalar.activation(f[:, :, u : u + P], acc[:], ACT.Tanh)
-            fg_planes = ring.tile([P, PACK, width], BF16, name="fg_planes", tag="fg_planes", align_bytes=64)
-            for t in range(PACK):
-                nc.scalar.activation(fg_planes[:, t, :], f[:, t, :], ACT.Copy, scale=gf_sb[:, t : t + 1])
-            fg_grouped = ring.tile([P, width, PACK], BF16, name="fg_grouped", tag="fg_grouped", align_bytes=64)
-            nc.scalar.copy(fg_grouped[:], fg_planes[:].rearrange("p t j -> p j t"))
-            return f, fg_grouped
 
-        def stage_out(j0, width, f, fg_grouped):
+        def stage_product(c):
+            width = CHUNKS[c]
+            fg_grouped = x_tiles[c][:, : 2 * width].bitcast(BF16)
+            nc.vector.tensor_tensor(
+                fg_grouped.rearrange("p (c i t) -> p c t i", i=PACK, t=PACK),
+                f_tiles[c][:].rearrange("p t (c i) -> p c t i", i=PACK),
+                gf_sb[:].unsqueeze(1).unsqueeze(3).to_broadcast([P, width // PACK, PACK, PACK]),
+                ALU.mult,
+            )
             codes = ring.tile([P, width], U32, name="fg_codes", tag="fg_codes", align_bytes=64)
             scales = ring.tile([P, width], U8, name="fg_scales", tag="fg_scales", align_bytes=64)
-            nc.vector.quantize_mx(
-                out=codes[:].bitcast(E4M3), scales=scales[:], in_=fg_grouped[:].rearrange("p j t -> p (j t)")
-            )
-            result = low_slot([P, PACK, width], F32, "result")
+            quantise((codes, scales), 0, width, fg_grouped)
             per_bank = BANK // width
+            y_banks[c] = []
             for t0 in range(0, PACK, per_bank):
                 acc = acc_bank([P, per_bank, width], "acc3")
+                y_banks[c].append(acc)
                 for t in range(t0, t0 + per_bank):
                     nc.tensor.matmul_mx(
                         out=acc[:, t - t0, :],
-                        lhsT=w3_q[t][0][:].bitcast(E4M3),
-                        lhsT_scale=w3_q[t][1][:],
+                        lhsT=w3_q[0][:, t * P : (t + 1) * P].bitcast(E4M3),
+                        lhsT_scale=w3_q[1][:, t * P : (t + 1) * P],
                         rhs=codes[:].bitcast(E4M3),
                         rhs_scale=scales[:],
                         start=True,
                         stop=True,
                     )
-                nc.vector.tensor_tensor(
-                    result[:, t0 : t0 + per_bank, :], acc[:], f[:, t0 : t0 + per_bank, :], ALU.add
-                )
-            nc.sync.dma_start(out_v[:, :, j0 : j0 + width], result[:])
 
-        starts = [sum(CHUNKS[:c]) for c in range(len(CHUNKS))]
-        made = {}
-        for c in range(len(CHUNKS) + 2):
-            if c < len(CHUNKS):
-                stage_pick(starts[c], CHUNKS[c])
-            if 1 <= c <= len(CHUNKS):
-                made[c - 1] = stage_features(starts[c - 1], CHUNKS[c - 1])
-            if c >= 2:
-                stage_out(starts[c - 2], CHUNKS[c - 2], *made[c - 2])
+        def stage_out(c):
+            j0, width = starts[c], CHUNKS[c]
+            result = z_tiles[c + 2] if c + 2 <= last else low_slot([P, S], F32, "result")
+            f_flat = f_tiles[c][:].rearrange("p t j -> p (t j)")
+            for k, acc in enumerate(y_banks[c]):
+                span = slice(k * BANK, (k + 1) * BANK)
+                nc.vector.tensor_tensor(
+                    result[:, span], acc[:].rearrange("p t j -> p (t j)"), f_flat[:, span], ALU.add
+                )
+            nc.sync.dma_start(
+                out_v[:, :, j0 : j0 + width], result[:, : PACK * width].rearrange("p (t j) -> p t j", t=PACK)
+            )
+
+        for step in range(-2, last + 2):
+            if step + 2 <= last:
+                stage_pick(step + 2)
+            if 0 <= step + 1 <= last:
+                stage_features(step + 1)
+            if 0 <= step - 1:
+                stage_out(step - 1)
+            if 0 <= step <= last:
+                stage_product(step)

@@ -22,12 +22,12 @@ PACK = 4
 PASS = P * PACK
 BANK = 512
 LIST = 16
+QUAD = 32
 KP = K // PASS
 HP = H // PASS
+PAIR = 2
+WIDE = 256
 CHUNKS = (128, 256, 256, 256, 128)
-FUSE_EARLY = True
-FUSE_LATE = True
-VECTOR_GAIN_FROM = 640
 
 
 def tile_list_moromi_panel_aroma_kernel(
@@ -40,42 +40,35 @@ def tile_list_moromi_panel_aroma_kernel(
         ring = ctx.enter_context(tc.tile_pool(name="ring", bufs=2))
         psum = ctx.enter_context(tc.psum_pool(name="psum", bufs=2))
 
-        def big(shape, dtype, name):
-            return ring.tile(shape, dtype, name=name, tag="big", bufs=3, align_bytes=64)
+        def slot(tag, bufs):
+            return lambda shape, dtype, name: ring.tile(shape, dtype, name=name, tag=tag, bufs=bufs, align_bytes=64)
 
-        def row(shape, name):
-            return ring.tile(shape, F32, name=name, tag="row", bufs=4, align_bytes=64)
-
-        def raw_weight(name):
-            return ring.tile([P, PACK, PASS], F32, name=name, tag="raw", bufs=3, align_bytes=64)
-
-        def early(shape, dtype, name):
-            return ring.tile(shape, dtype, name=name, tag="early", bufs=4, align_bytes=64)
-
-        def low_slot(shape, dtype, name):
-            return ring.tile(shape, dtype, name=name, tag="low", bufs=3, align_bytes=64)
+        big_slot = slot("big", KP)
+        raw_slot = slot("raw", KP)
+        grouped_slot = slot("grouped", KP)
+        row_slot = slot("row", PACK)
+        gain_slot = slot("gain", PACK)
+        low_slot = slot("low", 3)
+        late_slot = slot("late", 3)
+        z_rows_slot = slot("z_rows", 3)
 
         def acc_bank(shape, name):
             return psum.tile(shape, F32, name=name, tag="acc", bufs=4)
 
-        def clock(ap):
-            tick = ring.tile([P, 1], F32, name="tick", tag="tick")
-            nc.gpsimd.tensor_copy(tick[:], ap)
+        def entries(offsets, j0, width):
+            return offsets[:, j0 // LIST : (j0 + width) // LIST]
 
-        def cols(lst, j0, width):
-            return lst[:, j0 // LIST : (j0 + width) // LIST]
-
-        tab_sc = early([P, T], U8, "tab_sc")
-        w2_sc_raw = ring.tile([P, HP, N], U8, name="w2_sc_raw", tag="late", bufs=3, align_bytes=64)
-        nc.vector.memset(tab_sc[:].bitcast(I32), 0)
-        nc.vector.memset(w2_sc_raw[:].rearrange("p a c -> p (a c)").bitcast(I32), 0)
+        tab_plane = gain_slot([P, T], U8, "tab_plane")
+        w2_plane = late_slot([P, HP, N], U8, "w2_plane")
+        nc.vector.memset(tab_plane[:].bitcast(I32), 0)
+        nc.vector.memset(w2_plane[:].rearrange("p a c -> p (a c)").bitcast(I32), 0)
 
         idx = lists.tile([P, S // LIST], U16, name="idx")
         idx2 = lists.tile([P, S // LIST], U16, name="idx2")
         idx3 = lists.tile([P, S // LIST], U16, name="idx3")
         nc.sync.dma_start(idx[:], offs)
 
-        w2_raw = ring.tile([P, HP, 2 * N], U8, name="w2_raw", tag="late", bufs=3, align_bytes=64)
+        w2_raw = late_slot([P, HP, 2 * N], U8, "w2_raw")
         ga_sb = keep.tile([P, HP, PACK], F32, name="ga_sb")
         gf_sb = keep.tile([P, PACK], F32, name="gf_sb")
         pages = [keep.tile([P, T2], F32, name="page%d" % t) for t in range(PACK)]
@@ -85,73 +78,68 @@ def tile_list_moromi_panel_aroma_kernel(
         make_identity(nc, ident[:])
 
         def load_table(a):
-            words = big([P, T], I32, "tab%d" % a)
+            words = big_slot([P, T], I32, "tab%d" % a)
             nc.sync.dma_start(words[:], tab_words[a].rearrange("p t i -> p (t i)").bitcast(I32))
             return words
 
         def load_weight(rows, name):
-            raw = raw_weight(name)
+            raw = raw_slot([P, PACK, PASS], F32, name)
             nc.sync.dma_start(raw[:], rows.rearrange("(p i) c -> p i c", i=PACK))
             return raw
 
-        def w1_rows(b, a):
-            return w1[a * PASS : (a + 1) * PASS, b * PASS : (b + 1) * PASS]
+        def load_w1(b, a):
+            return load_weight(w1[a * PASS : (a + 1) * PASS, b * PASS : (b + 1) * PASS], "w1_%d%d" % (b, a))
 
-        lim_v = lim.rearrange("(b p i) j -> b p i j", b=HP, i=PACK)
-        clim_v = clim.rearrange("(b p i) j -> b p i j", b=HP, i=PACK)
+        lim_v = lim.rearrange("(b p t) j -> b p t j", b=HP, t=PACK)
+        clim_v = clim.rearrange("(b p t) j -> b p t j", b=HP, t=PACK)
         tab = {}
         w1_raw = {}
         tab[0] = load_table(0)
-        tab_sc_rows = early([P, T // 4], I32, "tab_sc_rows")
-        for q in range(4):
-            rows = slice(32 * q, 32 * q + 4 * KP)
-            nc.sync.dma_start(tab_sc_rows[rows, :], tab_scales[:, 4 * q : 4 * q + 4, :].bitcast(I32))
-            nc.vector.tensor_copy(tab_sc[rows, :].bitcast(I32), tab_sc_rows[rows, :])
-        nc.sync.dma_start(ga_sb[:], ga.rearrange("(b p i) -> p b i", b=HP, i=PACK))
-        warm = keep.tile([P, 1], F32, name="warm")
-        nc.scalar.activation(warm[:], ga_sb[:, 0, 0:1], ACT.Tanh)
-        w1_raw[0, 0] = load_weight(w1_rows(0, 0), "w1_00")
+        tab_rows = gain_slot([P, T // 4], I32, "tab_rows")
+        for q in range(P // QUAD):
+            live = slice(QUAD * q, QUAD * q + 4 * KP)
+            nc.sync.dma_start(tab_rows[live, :], tab_scales[:, 4 * q : 4 * q + 4, :].bitcast(I32))
+            nc.vector.tensor_copy(tab_plane[live, :].bitcast(I32), tab_rows[live, :])
+        nc.sync.dma_start(ga_sb[:], ga.rearrange("(b p t) -> p b t", b=HP, t=PACK))
+        w1_raw[0, 0] = load_w1(0, 0)
         tab[1] = load_table(1)
         nc.sync.dma_start(w2_raw[:].bitcast(I32), w2_words.rearrange("a p c -> p a c").bitcast(I32))
-        w2_sc_rows = ring.tile([P, HP, N // 4], I32, name="w2_sc_rows", tag="late", bufs=3, align_bytes=64)
-        for q in range(4):
-            rows = slice(32 * q, 32 * q + 4)
+        w2_rows = late_slot([P, HP, N // 4], I32, "w2_rows")
+        for q in range(P // QUAD):
+            live = slice(QUAD * q, QUAD * q + 4)
             nc.sync.dma_start(
-                w2_sc_rows[rows, :, :], w2_scales[:, 4 * q : 4 * q + 4, :].rearrange("a r c -> r a c").bitcast(I32)
+                w2_rows[live, :, :], w2_scales[:, 4 * q : 4 * q + 4, :].rearrange("a r c -> r a c").bitcast(I32)
             )
-            nc.vector.tensor_copy(w2_sc_raw[rows, :, :].bitcast(I32), w2_sc_rows[rows, :, :])
-        nc.sync.dma_start(gf_sb[:], gf.rearrange("(p i) -> p i", i=PACK))
-        w1_raw[0, 1] = load_weight(w1_rows(0, 1), "w1_01")
+            nc.vector.tensor_copy(w2_plane[live, :, :].bitcast(I32), w2_rows[live, :, :])
+        nc.sync.dma_start(gf_sb[:], gf.rearrange("(p t) -> p t", t=PACK))
+        w1_raw[0, 1] = load_w1(0, 1)
         tab[2] = load_table(2)
-        w1_raw[0, 2] = load_weight(w1_rows(0, 2), "w1_02")
+        w1_raw[0, 2] = load_w1(0, 2)
         wgs_sb = keep.tile([P, S], F32, name="wgs_sb")
         wgt_sb = keep.tile([P, S], F32, name="wgt_sb")
+        halves = [slice(h * BANK, (h + 1) * BANK) for h in range(S // BANK)]
         lim_sb = {}
-        lim_sb[0, 0] = row([P, S], "lim00")
-        for h in range(2):
-            half = slice(h * BANK, (h + 1) * BANK)
+        lim_sb[0, 0] = row_slot([P, S], F32, "lim00")
+        for h, half in enumerate(halves):
             nc.sync.dma_start(wgs_sb[:, half], wgs[:, half])
             nc.sync.dma_start(lim_sb[0, 0][:, half], lim_v[0, :, 0, half])
             if h == 0:
                 nc.sync.dma_start(idx2[:], offs2)
         for t in range(1, PACK):
-            lim_sb[0, t] = row([P, S], "lim0%d" % t)
+            lim_sb[0, t] = row_slot([P, S], F32, "lim0%d" % t)
             nc.sync.dma_start(lim_sb[0, t][:], lim_v[0, :, t, :])
         nc.sync.dma_start(idx3[:], offs3)
         nc.sync.dma_start(wgt_sb[:], wgt)
 
-        v_sc = keep.tile([P, S], U8, name="v_sc", align_bytes=64)
-        nc.vector.tensor_copy(v_sc[:], tab_sc[:].indirect(idx[:]))
+        v_scales = keep.tile([P, S], U8, name="v_scales", align_bytes=64)
+        nc.vector.tensor_copy(v_scales[:], tab_plane[:].indirect(idx[:]))
         v_codes = {}
         for a in range(KP):
-            for h in range(2):
+            for h in range(len(halves)):
                 v_codes[a, h] = keep.tile([P, BANK], U32, name="v%d%d" % (a, h), align_bytes=64)
                 nc.vector.tensor_copy(
-                    v_codes[a, h][:], tab[a][:].bitcast(U32).indirect(cols(idx, h * BANK, BANK))
+                    v_codes[a, h][:], tab[a][:].bitcast(U32).indirect(entries(idx, h * BANK, BANK))
                 )
-
-        def grouped_tile(name):
-            return ring.tile([P, PACK * PASS], BF16, name=name, tag="grouped", bufs=3, align_bytes=64)
 
         def round_weight_slice(grouped, raw, t):
             nc.scalar.copy(
@@ -164,65 +152,63 @@ def tile_list_moromi_panel_aroma_kernel(
             scales = keep.tile([P, width], U8, name=name + "_scales", align_bytes=64)
             return codes, scales
 
-        def quantise(dst, c0, width, grouped):
+        def quantise(dst, col0, width, grouped):
             codes, scales = dst
             nc.vector.quantize_mx(
-                out=codes[:, c0 : c0 + width].bitcast(E4M3), scales=scales[:, c0 : c0 + width], in_=grouped
+                out=codes[:, col0 : col0 + width].bitcast(E4M3), scales=scales[:, col0 : col0 + width], in_=grouped
             )
+
+        def make_gain(dst, b, t, span):
+            nc.scalar.activation(dst[:, span], wgs_sb[:, span], ACT.Copy, scale=ga_sb[:, b, t : t + 1])
 
         w1_q = {(b, a): operand(PASS, "w1q%d%d" % (b, a)) for b in range(HP) for a in range(KP)}
         gain = {}
         for a in range(KP):
-            grouped = grouped_tile("w1g0%d" % a)
+            grouped = grouped_slot([P, PACK * PASS], BF16, "w1g0%d" % a)
             for t in range(PACK):
                 round_weight_slice(grouped, w1_raw[0, a], t)
                 if a == KP - 1:
                     quantise(w1_q[0, a], t * P, P, grouped[:, t * PASS : (t + 1) * PASS])
-                    gain[0, t] = early([P, S], F32, "gain0%d" % t)
-                    for h in range(2):
-                        half = slice(h * BANK, (h + 1) * BANK)
-                        nc.scalar.activation(
-                            gain[0, t][:, half], wgs_sb[:, half], ACT.Copy, scale=ga_sb[:, 0, t : t + 1]
-                        )
+                    gain[0, t] = gain_slot([P, S], F32, "gain0%d" % t)
+                    for half in halves:
+                        make_gain(gain[0, t], 0, t, half)
             if a < KP - 1:
                 quantise(w1_q[0, a], 0, PASS, grouped[:])
 
         w2_codes = keep.tile([P, HP, PACK, P, 2], U8, name="w2_codes", align_bytes=64)
-        w2_sc = keep.tile([P, HP, PACK, P], U8, name="w2_sc", align_bytes=64)
+        w2_dealt = keep.tile([P, HP, PACK, P], U8, name="w2_dealt", align_bytes=64)
         nc.vector.tensor_copy(
             w2_codes[:].rearrange("p a t q e -> p a t (q e)").bitcast(U16),
             w2_raw[:].bitcast(U16).rearrange("p a (q t) -> p a t q", t=PACK),
         )
-        nc.vector.tensor_copy(w2_sc[:], w2_sc_raw[:].rearrange("p a (q t) -> p a t q", t=PACK))
+        nc.vector.tensor_copy(w2_dealt[:], w2_plane[:].rearrange("p a (q t) -> p a t q", t=PACK))
 
         for a in range(KP):
-            w1_raw[1, a] = load_weight(w1_rows(1, a), "w1_1%d" % a)
-        lim1 = big([P, PACK, S], F32, "lim1")
+            w1_raw[1, a] = load_w1(1, a)
+        lim1 = big_slot([P, PACK, S], F32, "lim1")
         nc.sync.dma_start(lim1[:], lim_v[1])
         for t in range(PACK):
             lim_sb[1, t] = lim1[:, t, :]
         clim_sb = {}
-        clim_sb[0] = big([P, PACK, S], F32, "clim0")
-        nc.sync.dma_start(clim_sb[0][:], clim_v[0])
-        clim_sb[1] = big([P, PACK, S], F32, "clim1")
-        nc.sync.dma_start(clim_sb[1][:], clim_v[1])
+        for b in range(HP):
+            clim_sb[b] = big_slot([P, PACK, S], F32, "clim%d" % b)
+            nc.sync.dma_start(clim_sb[b][:], clim_v[b])
 
-        w1_rounded = {}
+        w1_grouped = {}
         for a in range(KP):
-            w1_rounded[a] = grouped_tile("w1g1%d" % a)
+            w1_grouped[a] = grouped_slot([P, PACK * PASS], BF16, "w1g1%d" % a)
             for t in range(PACK):
-                round_weight_slice(w1_rounded[a], w1_raw[1, a], t)
-        for t0 in range(0, PACK, 2):
-            two = ring.tile([P, 2, S], F32, name="gain1%d" % t0, tag="raw", bufs=3, align_bytes=64)
-            for t in range(t0, t0 + 2):
-                gain[1, t] = two[:, t - t0, :]
-                nc.scalar.activation(gain[1, t], wgs_sb[:], ACT.Copy, scale=ga_sb[:, 1, t : t + 1])
+                round_weight_slice(w1_grouped[a], w1_raw[1, a], t)
+        for u in range(PACK // PAIR):
+            gains = raw_slot([P, PAIR, S], F32, "gain1%d" % u)
+            for e in range(PAIR):
+                gain[1, PAIR * u + e] = gains[:, e, :]
+                make_gain(gains[:, e, :], 1, PAIR * u + e, slice(0, S))
         w3_raw = load_weight(w3, "w3_raw")
 
         def capped(b, t):
             low = low_slot([P, S], F32, "low")
-            for h in range(2):
-                half = slice(h * BANK, (h + 1) * BANK)
+            for h, half in enumerate(halves):
                 acc = acc_bank([P, BANK], "acc1")
                 for a in range(KP):
                     codes, scales = w1_q[b, a]
@@ -231,113 +217,129 @@ def tile_list_moromi_panel_aroma_kernel(
                         lhsT=codes[:, t * P : (t + 1) * P].bitcast(E4M3),
                         lhsT_scale=scales[:, t * P : (t + 1) * P],
                         rhs=v_codes[a, h][:].bitcast(E4M3),
-                        rhs_scale=v_sc[4 * a : P, half],
+                        rhs_scale=v_scales[4 * a : P, half],
                         start=(a == 0),
                         stop=(a == KP - 1),
                     )
                 nc.vector.tensor_tensor(low[:, half], acc[:], lim_sb[b, t][:, half], ALU.min)
-            return low, gain[b, t]
+            return low
 
-        def put(t, low, factor, pieces):
-            width = S // pieces
+        def put(b, t, low, width):
             for j0 in range(0, S, width):
                 span = slice(j0, j0 + width)
                 nc.vector.tensor_tensor(
-                    pages[t][:].indirect(cols(idx2, j0, width)), low[:, span], factor[:, span], ALU.mult
+                    pages[t][:].indirect(entries(idx2, j0, width)), low[:, span], gain[b, t][:, span], ALU.mult
                 )
 
-        def pick(t, dst, j0, width, fused):
-            picked = pages[t][:].indirect(cols(idx3, j0, width))
-            if fused:
-                nc.vector.tensor_tensor(dst, picked, wgt_sb[:, j0 : j0 + width], ALU.mult)
-            else:
-                nc.vector.tensor_copy(dst, picked)
-                nc.gpsimd.tensor_tensor(dst, dst, wgt_sb[:, j0 : j0 + width], ALU.mult)
+        def pick(t, dst, j0, width):
+            nc.vector.tensor_tensor(
+                dst, pages[t][:].indirect(entries(idx3, j0, width)), wgt_sb[:, j0 : j0 + width], ALU.mult
+            )
 
-        z_q = {}
-
-        def round_z(b, j0, x_blocks, z_grouped):
-            total = psum.tile([P, PACK, P], F32, name="total", tag="total")
-            for t in range(PACK):
-                nc.tensor.matmul(
-                    total[:, t, :], clim_sb[b][:, t, j0 : j0 + P], ident[:],
-                    start=(t == 0), stop=False, is_transpose=True,
-                )
-            for t in range(PACK):
-                nc.tensor.matmul(
-                    total[:, t, :], x_blocks[t], ident[:], start=False, stop=(t == PACK - 1), is_transpose=True
-                )
-            z_rows = ring.tile([P, 2, P, 2], BF16, name="z_rows", tag="z_rows", align_bytes=64)
-            nc.scalar.copy(z_rows[:], total[:].rearrange("j (u e) p -> j u p e", e=2))
-            pairs = psum.tile([P, 2, P], F32, name="pairs", tag="pairs")
-            z_words = z_rows[:].rearrange("j u p e -> j (u p e)").bitcast(F32)
-            for u in range(2):
-                nc.tensor.transpose(pairs[:, u, :], z_words[:, u * P : (u + 1) * P], ident[:])
+        def round_pair(b, u, j0, width, x_pair, z_rows):
+            blocks = width // P
+            total = psum.tile([P, blocks, PAIR, P], F32, name="total", tag="total")
+            terms = [clim_sb[b][:, PAIR * u + e, j0 : j0 + width] for e in range(PAIR)] + x_pair
+            for i, term in enumerate(terms):
+                for blk in range(blocks):
+                    nc.tensor.matmul(
+                        total[:, blk, i % PAIR, :],
+                        term[:, blk * P : (blk + 1) * P],
+                        ident[:],
+                        start=(i == 0 and blk == 0),
+                        stop=(i == len(terms) - 1 and blk == blocks - 1),
+                        is_transpose=True,
+                    )
             nc.scalar.copy(
-                z_grouped.bitcast(F32).rearrange("p (j u) -> p j u", u=2), pairs[:].rearrange("p u j -> p j u")
+                z_rows.rearrange("j (blk p e) -> j blk p e", p=P, e=PAIR), total[:].rearrange("j blk e p -> j blk p e")
+            )
+
+        def group_z(width, z_rows, z_grouped):
+            blocks = width // P
+            pairs = psum.tile([P, blocks, PACK // PAIR, P], F32, name="pairs", tag="pairs")
+            for blk in range(blocks):
+                for u in range(PACK // PAIR):
+                    nc.tensor.transpose(
+                        pairs[:, blk, u, :], z_rows[u].bitcast(F32)[:, blk * P : (blk + 1) * P], ident[:]
+                    )
+            nc.scalar.copy(
+                z_grouped.bitcast(F32).rearrange("p (blk j u) -> p blk j u", j=P, u=PACK // PAIR),
+                pairs[:].rearrange("p blk u j -> p blk j u"),
             )
 
         order = [(b, t) for b in range(HP) for t in range(PACK)]
-        x0 = {}
+        x_whole = {}
+        z_q = {}
         w3_q = operand(N, "w3q")
-        ready = capped(0, 0)
+        low_next = capped(0, 0)
         for n, (b, t) in enumerate(order):
-            current = ready
-            if n == PACK - 1:
+            low_now = low_next
+            if n + 1 == PACK:
                 for a in range(KP):
-                    quantise(w1_q[1, a], 0, PASS, w1_rounded[a][:])
+                    quantise(w1_q[1, a], 0, PASS, w1_grouped[a][:])
             if n + 1 < len(order):
-                ready = capped(*order[n + 1])
-            put(t, current[0], current[1], 2 if n == 0 else 1)
-            if 1 <= n <= PACK:
-                x0[n - 1] = row([P, S], "x0%d" % (n - 1))
-                pick(n - 1, x0[n - 1][:], 0, S, FUSE_EARLY)
+                low_next = capped(*order[n + 1])
+            if 1 <= n <= PACK + PAIR:
+                before = order[n - 1]
+                x_whole[before] = (row_slot if before[0] == 0 else grouped_slot)([P, S], F32, "x%d%d" % before)
+                pick(before[1], x_whole[before][:], 0, S)
+            put(b, t, low_now, BANK if n == 0 else S)
             if n == PACK:
-                z0 = keep.tile([P, S * PACK], BF16, name="z0", align_bytes=64)
-                for j0 in range(0, S, P):
-                    blocks = [x0[i][:, j0 : j0 + P] for i in range(PACK)]
-                    round_z(0, j0, blocks, z0[:, j0 * PACK : (j0 + P) * PACK])
-            if n == len(order) - 2:
+                z0_grouped = keep.tile([P, S * PACK], BF16, name="z0_grouped", align_bytes=64)
+                for j0 in range(0, S, WIDE):
+                    z_rows = [z_rows_slot([P, PAIR * WIDE], BF16, "z_rows") for u in range(PACK // PAIR)]
+                    for u in range(PACK // PAIR):
+                        x_pair = [x_whole[0, PAIR * u + e][:, j0 : j0 + WIDE] for e in range(PAIR)]
+                        round_pair(0, u, j0, WIDE, x_pair, z_rows[u][:])
+                    group_z(WIDE, [tile[:] for tile in z_rows], z0_grouped[:, j0 * PACK : (j0 + WIDE) * PACK])
+            if n == PACK + PAIR:
                 z_q[0] = (
-                    ring.tile([P, S], U32, name="z0_codes", tag="row", bufs=4, align_bytes=64),
+                    row_slot([P, S], U32, "z0_codes"),
                     keep.tile([P, S], U8, name="z0_scales", align_bytes=64),
                 )
                 z_q[1] = (
                     low_slot([P, S], U32, "z1_codes"),
                     keep.tile([P, S], U8, name="z1_scales", align_bytes=64),
                 )
-                quantise(z_q[0], 0, S, z0[:])
-                w3_grouped = grouped_tile("w3g")
+                quantise(z_q[0], 0, S, z0_grouped[:])
+                w3_grouped = grouped_slot([P, PACK * PASS], BF16, "w3g")
                 for i in range(PACK):
                     round_weight_slice(w3_grouped, w3_raw, i)
                 quantise(w3_q, 0, N, w3_grouped[:])
-                x_first = row([P, S], "x1")
-                for i in range(PACK - 1):
-                    pick(i, x_first[:, i * CHUNKS[0] : (i + 1) * CHUNKS[0]], 0, CHUNKS[0], True)
+                z1_first_pair = keep.tile([P, PAIR * S], BF16, name="z1_first_pair", align_bytes=64)
+                for j0 in range(0, S, WIDE):
+                    x_pair = [x_whole[1, e][:, j0 : j0 + WIDE] for e in range(PAIR)]
+                    round_pair(1, 0, j0, WIDE, x_pair, z1_first_pair[:, PAIR * j0 : PAIR * (j0 + WIDE)])
+                x_first = row_slot([P, S], F32, "x_chunk")
+                pick(PAIR, x_first[:, : CHUNKS[0]], 0, CHUNKS[0])
 
         out_v = out.rearrange("(p t) j -> p t j", t=PACK)
-
         starts = [sum(CHUNKS[:c]) for c in range(len(CHUNKS))]
         last = len(CHUNKS) - 1
         x_tiles, z_tiles, f_tiles, y_banks = {}, {}, {}, {}
 
         def stage_pick(c):
             j0, width = starts[c], CHUNKS[c]
-            x = x_first if c == 0 else row([P, S], "x1")
+            x = x_first if c == 0 else row_slot([P, S], F32, "x_chunk")
             x_tiles[c] = x
-            for t in range(PACK - 1 if c == 0 else 0, PACK):
-                pick(t, x[:, t * width : (t + 1) * width], j0, width, True)
-            z_tiles[c] = ring.tile([P, S], F32, name="z1", tag="late", bufs=3, align_bytes=64)
-            for u in range(0, width, P):
-                blocks = [x[:, t * width + u : t * width + u + P] for t in range(PACK)]
-                round_z(1, j0 + u, blocks, z_tiles[c][:, 2 * u : 2 * (u + P)].bitcast(BF16))
+            x_pair = [x[:, e * width : (e + 1) * width] for e in range(PAIR)]
+            for e in range(1 if c == 0 else 0, PAIR):
+                pick(PAIR + e, x_pair[e], j0, width)
+            z_tiles[c] = late_slot([P, S], F32, "z1_grouped")
+            z_rows = z_rows_slot([P, PAIR * width], BF16, "z_rows")
+            round_pair(1, 1, j0, width, x_pair, z_rows[:])
+            group_z(
+                width,
+                [z1_first_pair[:, PAIR * j0 : PAIR * (j0 + width)], z_rows[:]],
+                z_tiles[c][:, : PAIR * width].bitcast(BF16),
+            )
 
         def stage_features(c):
             j0, width = starts[c], CHUNKS[c]
-            quantise(z_q[1], j0, width, z_tiles[c][:, : 2 * width].bitcast(BF16))
-            f = early([P, PACK, width], F32, "f")
+            quantise(z_q[1], j0, width, z_tiles[c][:, : PAIR * width].bitcast(BF16))
+            f = gain_slot([P, PACK, width], F32, "f")
             f_tiles[c] = f
-            for u in range(0, width, P):
+            for j in range(0, width, P):
                 acc = acc_bank([P, PACK, P], "acc2")
                 for t in range(PACK):
                     for b in range(HP):
@@ -345,20 +347,20 @@ def tile_list_moromi_panel_aroma_kernel(
                         nc.tensor.matmul_mx(
                             out=acc[:, t, :],
                             lhsT=w2_codes[:, b, t, :, :].rearrange("p q e -> p (q e)").bitcast(E2M1),
-                            lhsT_scale=w2_sc[:, b, t, :],
-                            rhs=codes[:, j0 + u : j0 + u + P].bitcast(E4M3),
-                            rhs_scale=scales[:, j0 + u : j0 + u + P],
+                            lhsT_scale=w2_dealt[:, b, t, :],
+                            rhs=codes[:, j0 + j : j0 + j + P].bitcast(E4M3),
+                            rhs_scale=scales[:, j0 + j : j0 + j + P],
                             start=(b == 0),
                             stop=(b == HP - 1),
                         )
-                nc.scalar.activation(f[:, :, u : u + P], acc[:], ACT.Tanh)
+                nc.scalar.activation(f[:, :, j : j + P], acc[:], ACT.Tanh)
 
         def stage_product(c):
             width = CHUNKS[c]
-            fg_grouped = x_tiles[c][:, : 2 * width].bitcast(BF16)
+            fg_grouped = x_tiles[c][:, : PAIR * width].bitcast(BF16)
             nc.vector.tensor_tensor(
-                fg_grouped.rearrange("p (c i t) -> p c t i", i=PACK, t=PACK),
-                f_tiles[c][:].rearrange("p t (c i) -> p c t i", i=PACK),
+                fg_grouped.rearrange("p (g i t) -> p g t i", i=PACK, t=PACK),
+                f_tiles[c][:].rearrange("p t (g i) -> p g t i", i=PACK),
                 gf_sb[:].unsqueeze(1).unsqueeze(3).to_broadcast([P, width // PACK, PACK, PACK]),
                 ALU.mult,
             )
@@ -385,14 +387,16 @@ def tile_list_moromi_panel_aroma_kernel(
             j0, width = starts[c], CHUNKS[c]
             result = z_tiles[c + 2] if c + 2 <= last else low_slot([P, S], F32, "result")
             f_flat = f_tiles[c][:].rearrange("p t j -> p (t j)")
-            for k, acc in enumerate(y_banks[c]):
-                span = slice(k * BANK, (k + 1) * BANK)
-                nc.vector.tensor_tensor(
-                    result[:, span], acc[:].rearrange("p t j -> p (t j)"), f_flat[:, span], ALU.add
+            y_flat = [acc[:].rearrange("p t j -> p (t j)") for acc in y_banks[c]]
+            for u in range(PACK // PAIR):
+                span = slice(PAIR * u * width, PAIR * (u + 1) * width)
+                y_pair = y_flat[span.start // BANK][:, span.start % BANK : span.start % BANK + PAIR * width]
+                nc.vector.tensor_tensor(result[:, span], y_pair, f_flat[:, span], ALU.add)
+                queue = nc.scalar if (c, u) == (last, PACK // PAIR - 1) else nc.sync
+                queue.dma_start(
+                    out_v[:, PAIR * u : PAIR * (u + 1), j0 : j0 + width],
+                    result[:, span].rearrange("p (t j) -> p t j", t=PAIR),
                 )
-            nc.sync.dma_start(
-                out_v[:, :, j0 : j0 + width], result[:, : PACK * width].rearrange("p (t j) -> p t j", t=PACK)
-            )
 
         for step in range(-2, last + 2):
             if step + 2 <= last:

from contextlib import ExitStack

import concourse.mybir as mybir
from concourse.masks import make_identity

K, H, N, T, S, T2 = 1536, 1024, 512, 4096, 1024, 2048
FLOPS = 2 * (K * H * S + H * N * S + N * N * S)

F32 = mybir.dt.float32
BF16 = mybir.dt.bfloat16
I32 = mybir.dt.int32
U32 = mybir.dt.uint32
U16 = mybir.dt.uint16
U8 = mybir.dt.uint8
E4M3 = mybir.dt.float8_e4m3fn_x4
E2M1 = mybir.dt.float4_e2m1fn_x4
ALU = mybir.AluOpType
ACT = mybir.ActivationFunctionType

P = 128
PACK = 4
PASS = P * PACK
BANK = 512
LIST = 16
QUAD = 32
KP = K // PASS
HP = H // PASS
PAIR = 2
WIDE = 256
CHUNKS = (128, 256, 256, 256, 128)


def tile_list_moromi_panel_aroma_kernel(
    tc, tab_words, tab_scales, offs, w1, lim, ga, offs2, wgs, offs3, wgt, clim, w2_words, w2_scales, gf, w3, out
):
    nc = tc.nc
    with ExitStack() as ctx:
        lists = ctx.enter_context(tc.tile_pool(name="lists", bufs=1))
        keep = ctx.enter_context(tc.tile_pool(name="keep", bufs=1))
        ring = ctx.enter_context(tc.tile_pool(name="ring", bufs=2))
        psum = ctx.enter_context(tc.psum_pool(name="psum", bufs=2))

        def slot(tag, bufs):
            return lambda shape, dtype, name: ring.tile(shape, dtype, name=name, tag=tag, bufs=bufs, align_bytes=64)

        big_slot = slot("big", KP)
        raw_slot = slot("raw", KP)
        grouped_slot = slot("grouped", KP)
        row_slot = slot("row", PACK)
        gain_slot = slot("gain", PACK)
        low_slot = slot("low", 3)
        late_slot = slot("late", 3)
        z_rows_slot = slot("z_rows", 3)

        def acc_bank(shape, name):
            return psum.tile(shape, F32, name=name, tag="acc", bufs=4)

        def entries(offsets, j0, width):
            return offsets[:, j0 // LIST : (j0 + width) // LIST]

        tab_plane = gain_slot([P, T], U8, "tab_plane")
        w2_plane = late_slot([P, HP, N], U8, "w2_plane")
        nc.vector.memset(tab_plane[:].bitcast(I32), 0)
        nc.vector.memset(w2_plane[:].rearrange("p a c -> p (a c)").bitcast(I32), 0)

        idx = lists.tile([P, S // LIST], U16, name="idx")
        idx2 = lists.tile([P, S // LIST], U16, name="idx2")
        idx3 = lists.tile([P, S // LIST], U16, name="idx3")
        nc.sync.dma_start(idx[:], offs)

        w2_raw = late_slot([P, HP, 2 * N], U8, "w2_raw")
        ga_sb = keep.tile([P, HP, PACK], F32, name="ga_sb")
        gf_sb = keep.tile([P, PACK], F32, name="gf_sb")
        pages = [keep.tile([P, T2], F32, name="page%d" % t) for t in range(PACK)]
        for t in range(PACK):
            nc.vector.memset(pages[t][:], 0.0)
        ident = keep.tile([P, P], F32, name="ident")
        make_identity(nc, ident[:])

        def load_table(a):
            words = big_slot([P, T], I32, "tab%d" % a)
            nc.sync.dma_start(words[:], tab_words[a].rearrange("p t i -> p (t i)").bitcast(I32))
            return words

        def load_weight(rows, name):
            raw = raw_slot([P, PACK, PASS], F32, name)
            nc.sync.dma_start(raw[:], rows.rearrange("(p i) c -> p i c", i=PACK))
            return raw

        def load_w1(b, a):
            return load_weight(w1[a * PASS : (a + 1) * PASS, b * PASS : (b + 1) * PASS], "w1_%d%d" % (b, a))

        lim_v = lim.rearrange("(b p t) j -> b p t j", b=HP, t=PACK)
        clim_v = clim.rearrange("(b p t) j -> b p t j", b=HP, t=PACK)
        tab = {}
        w1_raw = {}
        tab[0] = load_table(0)
        tab_rows = gain_slot([P, T // 4], I32, "tab_rows")
        for q in range(P // QUAD):
            live = slice(QUAD * q, QUAD * q + 4 * KP)
            nc.sync.dma_start(tab_rows[live, :], tab_scales[:, 4 * q : 4 * q + 4, :].bitcast(I32))
            nc.vector.tensor_copy(tab_plane[live, :].bitcast(I32), tab_rows[live, :])
        nc.sync.dma_start(ga_sb[:], ga.rearrange("(b p t) -> p b t", b=HP, t=PACK))
        w1_raw[0, 0] = load_w1(0, 0)
        tab[1] = load_table(1)
        nc.sync.dma_start(w2_raw[:].bitcast(I32), w2_words.rearrange("a p c -> p a c").bitcast(I32))
        w2_rows = late_slot([P, HP, N // 4], I32, "w2_rows")
        for q in range(P // QUAD):
            live = slice(QUAD * q, QUAD * q + 4)
            nc.sync.dma_start(
                w2_rows[live, :, :], w2_scales[:, 4 * q : 4 * q + 4, :].rearrange("a r c -> r a c").bitcast(I32)
            )
            nc.vector.tensor_copy(w2_plane[live, :, :].bitcast(I32), w2_rows[live, :, :])
        nc.sync.dma_start(gf_sb[:], gf.rearrange("(p t) -> p t", t=PACK))
        w1_raw[0, 1] = load_w1(0, 1)
        tab[2] = load_table(2)
        w1_raw[0, 2] = load_w1(0, 2)
        wgs_sb = keep.tile([P, S], F32, name="wgs_sb")
        wgt_sb = keep.tile([P, S], F32, name="wgt_sb")
        halves = [slice(h * BANK, (h + 1) * BANK) for h in range(S // BANK)]
        lim_sb = {}
        lim_sb[0, 0] = row_slot([P, S], F32, "lim00")
        for h, half in enumerate(halves):
            nc.sync.dma_start(wgs_sb[:, half], wgs[:, half])
            nc.sync.dma_start(lim_sb[0, 0][:, half], lim_v[0, :, 0, half])
            if h == 0:
                nc.sync.dma_start(idx2[:], offs2)
        for t in range(1, PACK):
            lim_sb[0, t] = row_slot([P, S], F32, "lim0%d" % t)
            nc.sync.dma_start(lim_sb[0, t][:], lim_v[0, :, t, :])
        nc.sync.dma_start(idx3[:], offs3)
        nc.sync.dma_start(wgt_sb[:], wgt)

        v_scales = keep.tile([P, S], U8, name="v_scales", align_bytes=64)
        nc.vector.tensor_copy(v_scales[:], tab_plane[:].indirect(idx[:]))
        v_codes = {}
        for a in range(KP):
            for h in range(len(halves)):
                v_codes[a, h] = keep.tile([P, BANK], U32, name="v%d%d" % (a, h), align_bytes=64)
                nc.vector.tensor_copy(
                    v_codes[a, h][:], tab[a][:].bitcast(U32).indirect(entries(idx, h * BANK, BANK))
                )

        def round_weight_slice(grouped, raw, t):
            nc.scalar.copy(
                grouped[:, t * PASS : (t + 1) * PASS].rearrange("p (q i) -> p q i", i=PACK),
                raw[:].rearrange("p i (q t) -> p t q i", t=PACK)[:, t, :, :],
            )

        def operand(width, name):
            codes = keep.tile([P, width], U32, name=name + "_codes", align_bytes=64)
            scales = keep.tile([P, width], U8, name=name + "_scales", align_bytes=64)
            return codes, scales

        def quantise(dst, col0, width, grouped):
            codes, scales = dst
            nc.vector.quantize_mx(
                out=codes[:, col0 : col0 + width].bitcast(E4M3), scales=scales[:, col0 : col0 + width], in_=grouped
            )

        def make_gain(dst, b, t, span):
            nc.scalar.activation(dst[:, span], wgs_sb[:, span], ACT.Copy, scale=ga_sb[:, b, t : t + 1])

        w1_q = {(b, a): operand(PASS, "w1q%d%d" % (b, a)) for b in range(HP) for a in range(KP)}
        gain = {}
        for a in range(KP):
            grouped = grouped_slot([P, PACK * PASS], BF16, "w1g0%d" % a)
            for t in range(PACK):
                round_weight_slice(grouped, w1_raw[0, a], t)
                if a == KP - 1:
                    quantise(w1_q[0, a], t * P, P, grouped[:, t * PASS : (t + 1) * PASS])
                    gain[0, t] = gain_slot([P, S], F32, "gain0%d" % t)
                    for half in halves:
                        make_gain(gain[0, t], 0, t, half)
            if a < KP - 1:
                quantise(w1_q[0, a], 0, PASS, grouped[:])

        w2_codes = keep.tile([P, HP, PACK, P, 2], U8, name="w2_codes", align_bytes=64)
        w2_dealt = keep.tile([P, HP, PACK, P], U8, name="w2_dealt", align_bytes=64)
        nc.vector.tensor_copy(
            w2_codes[:].rearrange("p a t q e -> p a t (q e)").bitcast(U16),
            w2_raw[:].bitcast(U16).rearrange("p a (q t) -> p a t q", t=PACK),
        )
        nc.vector.tensor_copy(w2_dealt[:], w2_plane[:].rearrange("p a (q t) -> p a t q", t=PACK))

        for a in range(KP):
            w1_raw[1, a] = load_w1(1, a)
        lim1 = big_slot([P, PACK, S], F32, "lim1")
        nc.sync.dma_start(lim1[:], lim_v[1])
        for t in range(PACK):
            lim_sb[1, t] = lim1[:, t, :]
        clim_sb = {}
        for b in range(HP):
            clim_sb[b] = big_slot([P, PACK, S], F32, "clim%d" % b)
            nc.sync.dma_start(clim_sb[b][:], clim_v[b])

        w1_grouped = {}
        for a in range(KP):
            w1_grouped[a] = grouped_slot([P, PACK * PASS], BF16, "w1g1%d" % a)
            for t in range(PACK):
                round_weight_slice(w1_grouped[a], w1_raw[1, a], t)
        for u in range(PACK // PAIR):
            gains = raw_slot([P, PAIR, S], F32, "gain1%d" % u)
            for e in range(PAIR):
                gain[1, PAIR * u + e] = gains[:, e, :]
                make_gain(gains[:, e, :], 1, PAIR * u + e, slice(0, S))
        w3_raw = load_weight(w3, "w3_raw")

        def capped(b, t):
            low = low_slot([P, S], F32, "low")
            for h, half in enumerate(halves):
                acc = acc_bank([P, BANK], "acc1")
                for a in range(KP):
                    codes, scales = w1_q[b, a]
                    nc.tensor.matmul_mx(
                        out=acc[:],
                        lhsT=codes[:, t * P : (t + 1) * P].bitcast(E4M3),
                        lhsT_scale=scales[:, t * P : (t + 1) * P],
                        rhs=v_codes[a, h][:].bitcast(E4M3),
                        rhs_scale=v_scales[4 * a : P, half],
                        start=(a == 0),
                        stop=(a == KP - 1),
                    )
                nc.vector.tensor_tensor(low[:, half], acc[:], lim_sb[b, t][:, half], ALU.min)
            return low

        def put(b, t, low, width):
            for j0 in range(0, S, width):
                span = slice(j0, j0 + width)
                nc.vector.tensor_tensor(
                    pages[t][:].indirect(entries(idx2, j0, width)), low[:, span], gain[b, t][:, span], ALU.mult
                )

        def pick(t, dst, j0, width):
            nc.vector.tensor_tensor(
                dst, pages[t][:].indirect(entries(idx3, j0, width)), wgt_sb[:, j0 : j0 + width], ALU.mult
            )

        def round_pair(b, u, j0, width, x_pair, z_rows):
            blocks = width // P
            total = psum.tile([P, blocks, PAIR, P], F32, name="total", tag="total")
            terms = [clim_sb[b][:, PAIR * u + e, j0 : j0 + width] for e in range(PAIR)] + x_pair
            for i, term in enumerate(terms):
                for blk in range(blocks):
                    nc.tensor.matmul(
                        total[:, blk, i % PAIR, :],
                        term[:, blk * P : (blk + 1) * P],
                        ident[:],
                        start=(i == 0 and blk == 0),
                        stop=(i == len(terms) - 1 and blk == blocks - 1),
                        is_transpose=True,
                    )
            nc.scalar.copy(
                z_rows.rearrange("j (blk p e) -> j blk p e", p=P, e=PAIR), total[:].rearrange("j blk e p -> j blk p e")
            )

        def group_z(width, z_rows, z_grouped):
            blocks = width // P
            pairs = psum.tile([P, blocks, PACK // PAIR, P], F32, name="pairs", tag="pairs")
            for blk in range(blocks):
                for u in range(PACK // PAIR):
                    nc.tensor.transpose(
                        pairs[:, blk, u, :], z_rows[u].bitcast(F32)[:, blk * P : (blk + 1) * P], ident[:]
                    )
            nc.scalar.copy(
                z_grouped.bitcast(F32).rearrange("p (blk j u) -> p blk j u", j=P, u=PACK // PAIR),
                pairs[:].rearrange("p blk u j -> p blk j u"),
            )

        order = [(b, t) for b in range(HP) for t in range(PACK)]
        x_whole = {}
        z_q = {}
        w3_q = operand(N, "w3q")
        low_next = capped(0, 0)
        for n, (b, t) in enumerate(order):
            low_now = low_next
            if n + 1 == PACK:
                for a in range(KP):
                    quantise(w1_q[1, a], 0, PASS, w1_grouped[a][:])
            if n + 1 < len(order):
                low_next = capped(*order[n + 1])
            if 1 <= n <= PACK + PAIR:
                before = order[n - 1]
                x_whole[before] = (row_slot if before[0] == 0 else grouped_slot)([P, S], F32, "x%d%d" % before)
                pick(before[1], x_whole[before][:], 0, S)
            put(b, t, low_now, BANK if n == 0 else S)
            if n == PACK:
                z0_grouped = keep.tile([P, S * PACK], BF16, name="z0_grouped", align_bytes=64)
                for j0 in range(0, S, WIDE):
                    z_rows = [z_rows_slot([P, PAIR * WIDE], BF16, "z_rows") for u in range(PACK // PAIR)]
                    for u in range(PACK // PAIR):
                        x_pair = [x_whole[0, PAIR * u + e][:, j0 : j0 + WIDE] for e in range(PAIR)]
                        round_pair(0, u, j0, WIDE, x_pair, z_rows[u][:])
                    group_z(WIDE, [tile[:] for tile in z_rows], z0_grouped[:, j0 * PACK : (j0 + WIDE) * PACK])
            if n == PACK + PAIR:
                z_q[0] = (
                    row_slot([P, S], U32, "z0_codes"),
                    keep.tile([P, S], U8, name="z0_scales", align_bytes=64),
                )
                z_q[1] = (
                    low_slot([P, S], U32, "z1_codes"),
                    keep.tile([P, S], U8, name="z1_scales", align_bytes=64),
                )
                quantise(z_q[0], 0, S, z0_grouped[:])
                w3_grouped = grouped_slot([P, PACK * PASS], BF16, "w3g")
                for i in range(PACK):
                    round_weight_slice(w3_grouped, w3_raw, i)
                quantise(w3_q, 0, N, w3_grouped[:])
                z1_first_pair = keep.tile([P, PAIR * S], BF16, name="z1_first_pair", align_bytes=64)
                for j0 in range(0, S, WIDE):
                    x_pair = [x_whole[1, e][:, j0 : j0 + WIDE] for e in range(PAIR)]
                    round_pair(1, 0, j0, WIDE, x_pair, z1_first_pair[:, PAIR * j0 : PAIR * (j0 + WIDE)])
                x_first = row_slot([P, S], F32, "x_chunk")
                pick(PAIR, x_first[:, : CHUNKS[0]], 0, CHUNKS[0])

        out_v = out.rearrange("(p t) j -> p t j", t=PACK)
        starts = [sum(CHUNKS[:c]) for c in range(len(CHUNKS))]
        last = len(CHUNKS) - 1
        x_tiles, z_tiles, f_tiles, y_banks = {}, {}, {}, {}

        def stage_pick(c):
            j0, width = starts[c], CHUNKS[c]
            x = x_first if c == 0 else row_slot([P, S], F32, "x_chunk")
            x_tiles[c] = x
            x_pair = [x[:, e * width : (e + 1) * width] for e in range(PAIR)]
            for e in range(1 if c == 0 else 0, PAIR):
                pick(PAIR + e, x_pair[e], j0, width)
            z_tiles[c] = late_slot([P, S], F32, "z1_grouped")
            z_rows = z_rows_slot([P, PAIR * width], BF16, "z_rows")
            round_pair(1, 1, j0, width, x_pair, z_rows[:])
            group_z(
                width,
                [z1_first_pair[:, PAIR * j0 : PAIR * (j0 + width)], z_rows[:]],
                z_tiles[c][:, : PAIR * width].bitcast(BF16),
            )

        def stage_features(c):
            j0, width = starts[c], CHUNKS[c]
            quantise(z_q[1], j0, width, z_tiles[c][:, : PAIR * width].bitcast(BF16))
            f = gain_slot([P, PACK, width], F32, "f")
            f_tiles[c] = f
            for j in range(0, width, P):
                acc = acc_bank([P, PACK, P], "acc2")
                for t in range(PACK):
                    for b in range(HP):
                        codes, scales = z_q[b]
                        nc.tensor.matmul_mx(
                            out=acc[:, t, :],
                            lhsT=w2_codes[:, b, t, :, :].rearrange("p q e -> p (q e)").bitcast(E2M1),
                            lhsT_scale=w2_dealt[:, b, t, :],
                            rhs=codes[:, j0 + j : j0 + j + P].bitcast(E4M3),
                            rhs_scale=scales[:, j0 + j : j0 + j + P],
                            start=(b == 0),
                            stop=(b == HP - 1),
                        )
                nc.scalar.activation(f[:, :, j : j + P], acc[:], ACT.Tanh)

        def stage_product(c):
            width = CHUNKS[c]
            fg_grouped = x_tiles[c][:, : PAIR * width].bitcast(BF16)
            nc.vector.tensor_tensor(
                fg_grouped.rearrange("p (g i t) -> p g t i", i=PACK, t=PACK),
                f_tiles[c][:].rearrange("p t (g i) -> p g t i", i=PACK),
                gf_sb[:].unsqueeze(1).unsqueeze(3).to_broadcast([P, width // PACK, PACK, PACK]),
                ALU.mult,
            )
            codes = ring.tile([P, width], U32, name="fg_codes", tag="fg_codes", align_bytes=64)
            scales = ring.tile([P, width], U8, name="fg_scales", tag="fg_scales", align_bytes=64)
            quantise((codes, scales), 0, width, fg_grouped)
            per_bank = BANK // width
            y_banks[c] = []
            for t0 in range(0, PACK, per_bank):
                acc = acc_bank([P, per_bank, width], "acc3")
                y_banks[c].append(acc)
                for t in range(t0, t0 + per_bank):
                    nc.tensor.matmul_mx(
                        out=acc[:, t - t0, :],
                        lhsT=w3_q[0][:, t * P : (t + 1) * P].bitcast(E4M3),
                        lhsT_scale=w3_q[1][:, t * P : (t + 1) * P],
                        rhs=codes[:].bitcast(E4M3),
                        rhs_scale=scales[:],
                        start=True,
                        stop=True,
                    )

        def stage_out(c):
            j0, width = starts[c], CHUNKS[c]
            result = z_tiles[c + 2] if c + 2 <= last else low_slot([P, S], F32, "result")
            f_flat = f_tiles[c][:].rearrange("p t j -> p (t j)")
            y_flat = [acc[:].rearrange("p t j -> p (t j)") for acc in y_banks[c]]
            for u in range(PACK // PAIR):
                span = slice(PAIR * u * width, PAIR * (u + 1) * width)
                y_pair = y_flat[span.start // BANK][:, span.start % BANK : span.start % BANK + PAIR * width]
                nc.vector.tensor_tensor(result[:, span], y_pair, f_flat[:, span], ALU.add)
                queue = nc.scalar if (c, u) == (last, PACK // PAIR - 1) else nc.sync
                queue.dma_start(
                    out_v[:, PAIR * u : PAIR * (u + 1), j0 : j0 + width],
                    result[:, span].rearrange("p (t j) -> p t j", t=PAIR),
                )

        for step in range(-2, last + 2):
            if step + 2 <= last:
                stage_pick(step + 2)
            if 0 <= step + 1 <= last:
                stage_features(step + 1)
            if 0 <= step - 1:
                stage_out(step - 1)
            if 0 <= step <= last:
                stage_product(step)
